import numpy as np
import ml_dtypes


def mxq(x, axis, fmt="e4m3"):
    dtype, down = {"e4m3": (ml_dtypes.float8_e4m3fn, 7), "e5m2": (ml_dtypes.float8_e5m2, 14)}[fmt]
    v = np.moveaxis(np.asarray(x, np.float32).astype(ml_dtypes.bfloat16).astype(np.float64), axis, -1)
    blocks = v.reshape(v.shape[:-1] + (-1, 32))
    amax = np.abs(blocks).max(-1, keepdims=True)
    byte = np.maximum(np.where(amax > 0, np.frexp(amax)[1] - 1 + 127, 0) - down, 1)
    scale = np.exp2(byte - 127.0)
    codes = (blocks / scale).astype(np.float32).astype(dtype).astype(np.float64)
    return np.moveaxis((codes * scale).reshape(v.shape), -1, axis)


WIDE = False


def mx_kscale(k):
    if not WIDE:
        return np.ones(k)
    levels = np.array([10, -10, 5, -5, 0])
    if k % 512:
        return np.exp2(np.random.permutation(np.resize(levels, k // 32))).repeat(32)
    a = np.empty((k // 512, 16))
    for p in range(k // 512):
        a[p, :8] = np.random.permutation(np.resize(levels, 8))
        for g in range(8):
            far = levels[np.abs(levels - a[p, g]) >= 10]
            a[p, g + 8] = far[np.random.randint(len(far))]
    return np.exp2(a.ravel()).repeat(32)


def f64(x):
    return np.asarray(x).astype(np.float64)


def striped(idx):
    return np.tile(idx.reshape(-1, 16).T, (8, 1)).astype(np.uint16)


def unstriped(offs):
    return offs[:16].T.reshape(-1).astype(np.int64)


E2M1 = np.array([0.0, 0.5, 1.0, 1.5, 2.0, 3.0, 4.0, 6.0, -0.0, -0.5, -1.0, -1.5, -2.0, -3.0, -4.0, -6.0])


def pack_weight(w, fmt):
    k, n = w.shape
    w = f64(np.asarray(w, np.float32).astype(ml_dtypes.bfloat16)).reshape(k // 32, 32, n)
    amax = np.abs(w).max(1)
    if fmt == "e4m3":
        byte = np.frexp(amax)[1] - 1 + 127 - 7
    else:
        mant, ex = np.frexp(amax / 6.0)
        byte = np.where(mant > 0.5, ex, ex - 1) + 127
    byte = np.clip(np.where(amax > 0, byte, 1), 1, 254)
    scaled = (w * np.exp2(127.0 - byte)[:, None, :]).reshape(k, n).astype(np.float32)
    by_word = np.ascontiguousarray(scaled.reshape(k // 512, 128, 4, n).transpose(0, 1, 3, 2))
    if fmt == "e4m3":
        words = by_word.astype(ml_dtypes.float8_e4m3fn).view(np.uint8)
    else:
        c = by_word.astype(ml_dtypes.float4_e2m1fn).view(np.uint8) & 0xF
        words = (c[..., 0::2] | (c[..., 1::2] << 4)).reshape(k // 512, 128, 2 * n)
    return np.ascontiguousarray(words), np.ascontiguousarray(byte.astype(np.uint8).reshape(k // 512, 16, n))


def unpack_weight(words, scales, fmt):
    g, _, n = scales.shape
    words = np.ascontiguousarray(words).reshape(g, 128, n, -1)
    if fmt == "e4m3":
        vals = words.view(ml_dtypes.float8_e4m3fn).astype(np.float64)
    else:
        nib = np.empty((g, 128, n, 4), np.uint8)
        nib[..., 0::2] = words & 0xF
        nib[..., 1::2] = words >> 4
        vals = E2M1[nib]
    vals = vals * np.repeat(np.exp2(scales.astype(np.float64) - 127.0), 8, axis=1)[..., None]
    return vals.transpose(0, 1, 3, 2).reshape(g * 512, n)


def gelu(v):
    return 0.5 * v * (1.0 + np.tanh(np.sqrt(2.0 / np.pi) * (v + 0.044715 * v**3)))


K, T, S, H, P, P2 = 1536, 4096, 1024, 1024, 512, 256


def setup_inputs():
    n = np.random.standard_normal
    s = mx_kscale(K)[:, None]
    u = mx_kscale(H)[:, None]
    tab_words, tab_scales = pack_weight(n((K, T)) * s, "e4m3")
    w1_words, w1_scales = pack_weight(1.4 * n((K, H)) / np.sqrt(K) / s, "e2m1")
    return {
        "tab_words": tab_words,
        "tab_scales": tab_scales,
        "offs": striped(np.random.permutation(T)[:S]),
        "pos1": striped(np.random.permutation(S)[:P]),
        "pos2": striped(np.random.permutation(S)[:P]),
        "pos3": striped(np.random.permutation(P)[:P2]),
        "pos4": striped(np.random.permutation(P)[:P2]),
        "w1_words": w1_words,
        "w1_scales": w1_scales,
        "gain": (np.exp(0.3 * n(H)) * u[:, 0]).astype(np.float32),
        "w2": (2.0 * n((H, H)) / np.sqrt(H) / u**2).astype(np.float32),
        "gr": (np.exp(0.3 * n(H)) / u[:, 0]).astype(np.float32),
    }


def reference(tab_words, tab_scales, offs, pos1, pos2, pos3, pos4, w1_words, w1_scales, gain, w2, gr):
    v = unpack_weight(tab_words, tab_scales, "e4m3")[:, unstriped(offs)]
    w1 = unpack_weight(w1_words, w1_scales, "e2m1")
    h = np.tanh(w1.T @ v) * f64(gain)[:, None]
    h1 = h[:, unstriped(pos1)]
    x = h1 * h[:, unstriped(pos2)]
    e = np.tanh(mxq(f64(w2), 0, "e4m3").T @ mxq(x, 0, "e4m3"))
    y = e + h1 * f64(gr)[:, None]
    return np.minimum(y[:, unstriped(pos3)], y[:, unstriped(pos4)])

@@ -1,0 +1,291 @@
+from contextlib import ExitStack
+
+import concourse.mybir as mybir
+
+K, T, S, H, PAIRS, KEPT = 1536, 4096, 1024, 1024, 512, 256
+FLOPS = 2 * K * H * S + 2 * H * H * PAIRS
+
+F32 = mybir.dt.float32
+BF16 = mybir.dt.bfloat16
+I32 = mybir.dt.int32
+U32 = mybir.dt.uint32
+U16 = mybir.dt.uint16
+U8 = mybir.dt.uint8
+FP8X4 = mybir.dt.float8_e4m3fn_x4
+FP4X4 = mybir.dt.float4_e2m1fn_x4
+ALU = mybir.AluOpType
+ACT = mybir.ActivationFunctionType
+
+P = 128
+PACK = 4
+BANK = 512
+PASSES1 = K // (P * PACK)
+PASSES2 = H // (P * PACK)
+SLICES = H // P
+QUADS = 4
+AHEAD = 4
+
+
+def tile_list_beetle_trap_pairs_kernel(
+    tc, tab_words, tab_scales, offs, pos1, pos2, pos3, pos4, w1_words, w1_scales, gain, w2, gr, out
+):
+    nc = tc.nc
+    with ExitStack() as ctx:
+        lists = ctx.enter_context(tc.tile_pool(name="lists", bufs=1))
+        sb = ctx.enter_context(tc.tile_pool(name="sb", bufs=1))
+        psum = ctx.enter_context(tc.psum_pool(name="psum", bufs=1))
+
+        def load_list(src, name):
+            t = lists.tile(list(src.shape), U16, name=name)
+            nc.sync.dma_start(t[:], src)
+            return t
+
+        def bank(index, name):
+            return psum.tile([P, BANK], F32, name=name, tag="bank%d" % index)
+
+        tab_sc_win = sb.tile([P, T], U8, name="tab_sc_win", align_bytes=64)
+        nc.vector.memset(tab_sc_win[:].bitcast(I32), 0)
+        w1_sc_raw = sb.tile([P, H], U8, name="w1_sc_raw", align_bytes=64)
+        nc.vector.memset(w1_sc_raw[:].bitcast(I32), 0)
+        planes = sb.tile([P, PASSES1, S + H], U8, name="planes", align_bytes=64)
+        nc.vector.memset(planes[:].rearrange("p a n -> p (a n)").bitcast(I32), 0)
+
+        packed_rows = slice(0, 2 * 16 * PASSES1, 2)
+        offs_t = load_list(offs, "offs_t")
+        w1_raw = sb.tile([P, PASSES1, 2 * H], U8, name="w1_raw", align_bytes=64)
+        nc.sync.dma_start(w1_raw[:].bitcast(I32), w1_words.rearrange("a p n -> p a n").bitcast(I32))
+        nc.sync.dma_start(tab_sc_win[packed_rows, :].bitcast(I32), tab_scales.rearrange("a q n -> q a n").bitcast(I32))
+        nc.sync.dma_start(w1_sc_raw[packed_rows, :].bitcast(I32), w1_scales.rearrange("a q n -> q a n").bitcast(I32))
+        windows = []
+
+        def load_window(a):
+            win = sb.tile([P, T], I32, name="win%d" % a, tag="big%d" % a, align_bytes=64)
+            nc.sync.dma_start(win[:], tab_words[a].rearrange("p t i -> p (t i)").bitcast(I32))
+            windows.append(win)
+
+        load_window(0)
+        pos1_t = load_list(pos1, "pos1_t")
+        pos2_t = load_list(pos2, "pos2_t")
+        pos3_t = load_list(pos3, "pos3_t")
+        pos4_t = load_list(pos4, "pos4_t")
+        for a in range(1, PASSES1):
+            load_window(a)
+        gain_t = sb.tile([P, PASSES2, PACK], F32, name="gain_t")
+        nc.gpsimd.dma_start(gain_t[:], gain.rearrange("(b p t) -> p b t", p=P, t=PACK))
+        gr_t = sb.tile([P, PASSES2, PACK], F32, name="gr_t")
+        nc.gpsimd.dma_start(gr_t[:], gr.rearrange("(b p t) -> p b t", p=P, t=PACK))
+
+        v_sc_picked = sb.tile([P, S], U8, name="v_sc_picked", align_bytes=64)
+        nc.vector.tensor_copy(v_sc_picked[:], tab_sc_win[:].indirect(offs_t[:]))
+        packed = sb.tile([P, S + H], U8, name="packed", align_bytes=64)
+        nc.vector.tensor_copy(
+            packed[:, S:].rearrange("p (b t q) -> p b t q", b=PASSES2, t=PACK),
+            w1_sc_raw[:].rearrange("p (b q t) -> p b t q", b=PASSES2, t=PACK),
+        )
+        nc.vector.tensor_copy(packed[:, :S].bitcast(I32), v_sc_picked[:].bitcast(I32))
+        rows = 2 * 4 * PASSES1
+        for q in range(QUADS):
+            nc.scalar.dma_start(
+                planes[32 * q : 32 * q + 4, :, :].bitcast(I32),
+                packed[rows * q : rows * (q + 1) : 2, :].bitcast(I32),
+            )
+
+        w1_codes = sb.tile([P, PASSES1, 2 * H], U8, name="w1_codes", align_bytes=64)
+        for a in range(PASSES1):
+            nc.vector.tensor_copy(
+                w1_codes[:, a, :].bitcast(U16).rearrange("p (b t q) -> p b t q", b=PASSES2, t=PACK),
+                w1_raw[:, a, :].bitcast(U16).rearrange("p (b q t) -> p b t q", b=PASSES2, t=PACK),
+            )
+
+        gain_sq = sb.tile([P, SLICES], F32, name="gain_sq")
+        skip_k = sb.tile([P, SLICES], F32, name="skip_k")
+        flat_gain = gain_t[:].rearrange("p b t -> p (b t)")
+        nc.gpsimd.tensor_tensor(gain_sq[:], flat_gain, flat_gain, ALU.mult)
+        nc.gpsimd.tensor_tensor(skip_k[:], flat_gain, gr_t[:].rearrange("p b t -> p (b t)"), ALU.mult)
+
+        halves = S // BANK
+        cols16 = BANK // 16
+        v_words = [sb.tile([P, S], U32, name="v_words%d" % a, align_bytes=64) for a in range(PASSES1)]
+        acc1 = {}
+
+        def stage1_pass(s, h, a):
+            if a == 0:
+                acc1[s, h] = bank(halves * (s % AHEAD) + h, "acc1")
+            cols = slice(h * BANK, (h + 1) * BANK)
+            nc.tensor.matmul_mx(
+                out=acc1[s, h][:],
+                lhsT=w1_codes[:, a, 2 * P * s : 2 * P * (s + 1)].bitcast(FP4X4),
+                lhsT_scale=planes[:, a, S + P * s : S + P * (s + 1)],
+                rhs=v_words[a][:, cols].bitcast(FP8X4),
+                rhs_scale=planes[:, a, cols],
+                start=(a == 0),
+                stop=(a == PASSES1 - 1),
+            )
+
+        last = PASSES1 - 1
+        for a in range(last):
+            nc.vector.tensor_copy(v_words[a][:], windows[a][:].bitcast(U32).indirect(offs_t[:]))
+            for s in range(AHEAD):
+                for h in range(halves):
+                    stage1_pass(s, h, a)
+        for h in range(halves):
+            nc.vector.tensor_copy(
+                v_words[last][:, h * BANK : (h + 1) * BANK],
+                windows[last][:].bitcast(U32).indirect(offs_t[:, h * cols16 : (h + 1) * cols16]),
+            )
+
+        w2_raw = []
+        for b in range(PASSES2):
+            raw = sb.tile([P, PACK, H], F32, name="w2_raw%d" % b, tag="big%d" % b, align_bytes=64)
+            nc.sync.dma_start(raw[:], w2[b * 512 : (b + 1) * 512, :].rearrange("(p j) n -> p j n", j=PACK))
+            w2_raw.append(raw)
+
+        tanh1, edge, edge_g2 = {}, {}, {}
+        x_f32 = [sb.tile([P, PACK, PAIRS], F32, name="x_f32_%d" % b) for b in range(PASSES2)]
+        x_bf = [sb.tile([P, PAIRS, PACK], BF16, name="x_bf%d" % b, align_bytes=64) for b in range(PASSES2)]
+        x_codes = [sb.tile([P, PAIRS], U32, name="x_codes%d" % b, align_bytes=64) for b in range(PASSES2)]
+        x_sc = [sb.tile([P, PAIRS], U8, name="x_sc%d" % b, align_bytes=64) for b in range(PASSES2)]
+
+        def features(s):
+            for h in range(halves):
+                for a in range(last if s < AHEAD else 0, PASSES1):
+                    stage1_pass(s, h, a)
+            tanh1[s] = sb.tile([P, S], F32, name="tanh1", bufs=4)
+            for h in range(halves):
+                nc.scalar.activation(tanh1[s][:, h * BANK : (h + 1) * BANK], acc1[s, h][:], ACT.Tanh)
+
+        def pick_edge(s):
+            edge[s] = sb.tile([P, PAIRS], F32, name="edge%d" % s)
+            nc.vector.tensor_copy(edge[s][:], tanh1[s][:].indirect(pos1_t[:]))
+
+        def scale_edge(s):
+            edge_g2[s] = sb.tile([P, PAIRS], F32, name="edge_g2", bufs=3)
+            nc.scalar.activation(edge_g2[s][:], edge[s][:], ACT.Copy, scale=gain_sq[:, s : s + 1])
+
+        def pick_interior(s):
+            b, t = divmod(s, PACK)
+            nc.vector.tensor_tensor(x_f32[b][:, t, :], tanh1[s][:].indirect(pos2_t[:]), edge_g2[s][:], ALU.mult)
+
+        def weave_x(b, engine_copy, part, parts):
+            w = PAIRS // parts
+            cols = slice(part * w, (part + 1) * w)
+            engine_copy(
+                x_bf[b][:, cols, :].rearrange("p (c i) t -> p c t i", i=4),
+                x_f32[b][:, :, cols].rearrange("p t (c i) -> p c t i", i=4),
+            )
+
+        def quantise_x(b):
+            nc.vector.quantize_mx(
+                out=x_codes[b][:].bitcast(FP8X4), scales=x_sc[b][:], in_=x_bf[b][:].rearrange("p m t -> p (m t)")
+            )
+
+        groups = SLICES // 2
+        w2_bf, w2_codes, w2_sc = {}, {}, {}
+
+        def round_w2(g, b):
+            c, tp = divmod(g, 2)
+            if b == 0:
+                w2_bf[g] = sb.tile([P, PASSES2, 2, P, PACK], BF16, name="w2_bf", bufs=2, align_bytes=64)
+            src = w2_raw[b][:, :, c * 512 : (c + 1) * 512].rearrange("p j (m t) -> p m j t", t=PACK)
+            nc.scalar.copy(w2_bf[g][:, b].rearrange("p u m j -> p m j u"), src[:, :, :, 2 * tp : 2 * tp + 2])
+
+        def quantise_w2(g):
+            w2_codes[g] = sb.tile([P, PASSES2 * 2 * P], U32, name="w2_codes%d" % g, align_bytes=64)
+            w2_sc[g] = sb.tile([P, PASSES2 * 2 * P], U8, name="w2_sc%d" % g, align_bytes=64)
+            nc.vector.quantize_mx(
+                out=w2_codes[g][:].bitcast(FP8X4),
+                scales=w2_sc[g][:],
+                in_=w2_bf[g][:].rearrange("p b u m j -> p (b u m j)"),
+            )
+
+        features(0)
+        features(1)
+        pick_edge(0)
+        for s in range(SLICES):
+            if s + 1 < SLICES:
+                pick_edge(s + 1)
+            scale_edge(s)
+            if s + 2 < SLICES:
+                features(s + 2)
+            pick_interior(s)
+            if s == 2:
+                round_w2(0, 0)
+            if s == 4:
+                weave_x(0, nc.scalar.copy, 0, 2)
+            if s == 5:
+                weave_x(0, nc.scalar.copy, 1, 2)
+                round_w2(0, 1)
+            if s == 6:
+                quantise_x(0)
+                quantise_w2(0)
+                round_w2(1, 0)
+
+        acc2, pair, y = {}, {}, {}
+
+        def stage2_pass(s, b):
+            g, u = divmod(s, 2)
+            if b == 0:
+                acc2[s] = bank(s, "acc2")
+            cols = slice((2 * b + u) * P, (2 * b + u + 1) * P)
+            nc.tensor.matmul_mx(
+                out=acc2[s][:],
+                lhsT=w2_codes[g][:, cols].bitcast(FP8X4),
+                lhsT_scale=w2_sc[g][:, cols],
+                rhs=x_codes[b][:].bitcast(FP8X4),
+                rhs_scale=x_sc[b][:],
+                start=(b == 0),
+                stop=(b == PASSES2 - 1),
+            )
+
+        def pair_features(s):
+            pair[s] = sb.tile([P, PAIRS], F32, name="pair", bufs=3)
+            nc.scalar.activation(pair[s][:], acc2[s][:], ACT.Tanh)
+
+        def add_skip(s):
+            y[s] = sb.tile([P, PAIRS], F32, name="y", bufs=3)
+            nc.vector.scalar_tensor_tensor(y[s][:], edge[s][:], skip_k[:, s : s + 1], pair[s][:], ALU.mult, ALU.add)
+
+        cand3, cand4 = {}, {}
+
+        def pick_candidates(s):
+            g, u = divmod(s, 2)
+            if u == 0:
+                cand3[g] = sb.tile([P, 2, KEPT], F32, name="cand3", bufs=2)
+                cand4[g] = sb.tile([P, 2, KEPT], F32, name="cand4", bufs=2)
+            nc.vector.tensor_copy(cand3[g][:, u, :], y[s][:].indirect(pos3_t[:]))
+            nc.vector.tensor_copy(cand4[g][:, u, :], y[s][:].indirect(pos4_t[:]))
+
+        out_rows = out.rearrange("(c p t) j -> c p t j", p=P, t=PACK)
+
+        def lesser(g):
+            c, tp = divmod(g, 2)
+            res = sb.tile([P, 2, KEPT], F32, name="res", bufs=2)
+            nc.vector.tensor_tensor(res[:], cand3[g][:], cand4[g][:], ALU.min)
+            nc.sync.dma_start(out_rows[c][:, 2 * tp : 2 * tp + 2, :], res[:])
+
+        stage2_pass(0, 0)
+        stage2_pass(1, 0)
+        weave_x(1, nc.vector.tensor_copy, 0, 1)
+        round_w2(1, 1)
+        quantise_x(1)
+        quantise_w2(1)
+        for s in range(2):
+            stage2_pass(s, 1)
+            pair_features(s)
+        add_skip(0)
+        for s in range(SLICES):
+            g, u = divmod(s, 2)
+            if s + 2 < SLICES:
+                stage2_pass(s + 2, 0)
+                stage2_pass(s + 2, 1)
+                pair_features(s + 2)
+            if g + 2 < groups:
+                round_w2(g + 2, u)
+            if s + 1 < SLICES:
+                add_skip(s + 1)
+            if u == 0 and g > 0:
+                lesser(g - 1)
+            pick_candidates(s)
+            if u == 1 and g + 2 < groups:
+                quantise_w2(g + 2)
+        lesser(groups - 1)

@@ -23,7 +23,8 @@ PASSES1 = K // (P * PACK)
 PASSES2 = H // (P * PACK)
 SLICES = H // P
 QUADS = 4
-AHEAD = 4
+AHEAD = 3
+RING = 3
 
 
 def tile_list_beetle_trap_pairs_kernel(
@@ -43,18 +44,21 @@ def tile_list_beetle_trap_pairs_kernel(
         def bank(index, name):
             return psum.tile([P, BANK], F32, name=name, tag="bank%d" % index)
 
-        tab_sc_win = sb.tile([P, T], U8, name="tab_sc_win", align_bytes=64)
-        nc.vector.memset(tab_sc_win[:].bitcast(I32), 0)
+        tab_sc_win = sb.tile([P, T], U8, name="tab_sc_win", tag="picked0", align_bytes=64)
         w1_sc_raw = sb.tile([P, H], U8, name="w1_sc_raw", align_bytes=64)
-        nc.vector.memset(w1_sc_raw[:].bitcast(I32), 0)
+        first_row = 48
+        end_row = first_row + 16 * PASSES1
+        for raw in (tab_sc_win, w1_sc_raw):
+            nc.vector.memset(raw[:first_row, :].bitcast(I32), 0)
+            nc.vector.memset(raw[end_row:, :].bitcast(I32), 0)
         planes = sb.tile([P, PASSES1, S + H], U8, name="planes", align_bytes=64)
         nc.vector.memset(planes[:].rearrange("p a n -> p (a n)").bitcast(I32), 0)
 
-        packed_rows = slice(0, 2 * 16 * PASSES1, 2)
+        packed_rows = slice(first_row, end_row)
         offs_t = load_list(offs, "offs_t")
+        nc.scalar.dma_start(tab_sc_win[packed_rows, :].bitcast(I32), tab_scales.rearrange("a q n -> q a n").bitcast(I32))
         w1_raw = sb.tile([P, PASSES1, 2 * H], U8, name="w1_raw", align_bytes=64)
         nc.sync.dma_start(w1_raw[:].bitcast(I32), w1_words.rearrange("a p n -> p a n").bitcast(I32))
-        nc.sync.dma_start(tab_sc_win[packed_rows, :].bitcast(I32), tab_scales.rearrange("a q n -> q a n").bitcast(I32))
         nc.sync.dma_start(w1_sc_raw[packed_rows, :].bitcast(I32), w1_scales.rearrange("a q n -> q a n").bitcast(I32))
         windows = []
 
@@ -63,19 +67,18 @@ def tile_list_beetle_trap_pairs_kernel(
             nc.sync.dma_start(win[:], tab_words[a].rearrange("p t i -> p (t i)").bitcast(I32))
             windows.append(win)
 
-        load_window(0)
         pos1_t = load_list(pos1, "pos1_t")
         pos2_t = load_list(pos2, "pos2_t")
         pos3_t = load_list(pos3, "pos3_t")
+        load_window(0)
         pos4_t = load_list(pos4, "pos4_t")
-        for a in range(1, PASSES1):
-            load_window(a)
+        load_window(1)
         gain_t = sb.tile([P, PASSES2, PACK], F32, name="gain_t")
         nc.gpsimd.dma_start(gain_t[:], gain.rearrange("(b p t) -> p b t", p=P, t=PACK))
         gr_t = sb.tile([P, PASSES2, PACK], F32, name="gr_t")
         nc.gpsimd.dma_start(gr_t[:], gr.rearrange("(b p t) -> p b t", p=P, t=PACK))
 
-        v_sc_picked = sb.tile([P, S], U8, name="v_sc_picked", align_bytes=64)
+        v_sc_picked = sb.tile([P, S], U8, name="v_sc_picked", tag="big2", align_bytes=64)
         nc.vector.tensor_copy(v_sc_picked[:], tab_sc_win[:].indirect(offs_t[:]))
         packed = sb.tile([P, S + H], U8, name="packed", align_bytes=64)
         nc.vector.tensor_copy(
@@ -83,12 +86,13 @@ def tile_list_beetle_trap_pairs_kernel(
             w1_sc_raw[:].rearrange("p (b q t) -> p b t q", b=PASSES2, t=PACK),
         )
         nc.vector.tensor_copy(packed[:, :S].bitcast(I32), v_sc_picked[:].bitcast(I32))
-        rows = 2 * 4 * PASSES1
+        rows = 4 * PASSES1
         for q in range(QUADS):
-            nc.scalar.dma_start(
+            (nc.scalar if q % 2 == 0 else nc.sync).dma_start(
                 planes[32 * q : 32 * q + 4, :, :].bitcast(I32),
-                packed[rows * q : rows * (q + 1) : 2, :].bitcast(I32),
+                packed[first_row + rows * q : first_row + rows * (q + 1), :].bitcast(I32),
             )
+        load_window(PASSES1 - 1)
 
         w1_codes = sb.tile([P, PASSES1, 2 * H], U8, name="w1_codes", align_bytes=64)
         for a in range(PASSES1):
@@ -105,12 +109,12 @@ def tile_list_beetle_trap_pairs_kernel(
 
         halves = S // BANK
         cols16 = BANK // 16
-        v_words = [sb.tile([P, S], U32, name="v_words%d" % a, align_bytes=64) for a in range(PASSES1)]
+        v_words = [sb.tile([P, S], U32, name="v_words%d" % a, tag="picked%d" % a, align_bytes=64) for a in range(PASSES1)]
         acc1 = {}
 
         def stage1_pass(s, h, a):
             if a == 0:
-                acc1[s, h] = bank(halves * (s % AHEAD) + h, "acc1")
+                acc1[s, h] = bank(halves * (s % RING) + h, "acc1")
             cols = slice(h * BANK, (h + 1) * BANK)
             nc.tensor.matmul_mx(
                 out=acc1[s, h][:],
@@ -136,7 +140,7 @@ def tile_list_beetle_trap_pairs_kernel(
 
         w2_raw = []
         for b in range(PASSES2):
-            raw = sb.tile([P, PACK, H], F32, name="w2_raw%d" % b, tag="big%d" % b, align_bytes=64)
+            raw = sb.tile([P, PACK, H], F32, name="w2_raw%d" % b, tag="big%d" % (b + 1), align_bytes=64)
             nc.sync.dma_start(raw[:], w2[b * 512 : (b + 1) * 512, :].rearrange("(p j) n -> p j n", j=PACK))
             w2_raw.append(raw)
 
@@ -150,7 +154,10 @@ def tile_list_beetle_trap_pairs_kernel(
             for h in range(halves):
                 for a in range(last if s < AHEAD else 0, PASSES1):
                     stage1_pass(s, h, a)
-            tanh1[s] = sb.tile([P, S], F32, name="tanh1", bufs=4)
+            if s < 2:
+                tanh1[s] = sb.tile([P, S], F32, name="tanh1", tag="stage%d" % s, align_bytes=64)
+            else:
+                tanh1[s] = sb.tile([P, S], F32, name="tanh1", bufs=3)
             for h in range(halves):
                 nc.scalar.activation(tanh1[s][:, h * BANK : (h + 1) * BANK], acc1[s, h][:], ACT.Tanh)
 
@@ -162,9 +169,12 @@ def tile_list_beetle_trap_pairs_kernel(
             edge_g2[s] = sb.tile([P, PAIRS], F32, name="edge_g2", bufs=3)
             nc.scalar.activation(edge_g2[s][:], edge[s][:], ACT.Copy, scale=gain_sq[:, s : s + 1])
 
-        def pick_interior(s):
+        def pick_interior(s, part, parts):
             b, t = divmod(s, PACK)
-            nc.vector.tensor_tensor(x_f32[b][:, t, :], tanh1[s][:].indirect(pos2_t[:]), edge_g2[s][:], ALU.mult)
+            w = PAIRS // parts
+            cols = slice(part * w, (part + 1) * w)
+            entries = pos2_t[:, part * w // 16 : (part + 1) * w // 16]
+            nc.vector.tensor_tensor(x_f32[b][:, t, cols], tanh1[s][:].indirect(entries), edge_g2[s][:, cols], ALU.mult)
 
         def weave_x(b, engine_copy, part, parts):
             w = PAIRS // parts
@@ -185,7 +195,7 @@ def tile_list_beetle_trap_pairs_kernel(
         def round_w2(g, b):
             c, tp = divmod(g, 2)
             if b == 0:
-                w2_bf[g] = sb.tile([P, PASSES2, 2, P, PACK], BF16, name="w2_bf", bufs=2, align_bytes=64)
+                w2_bf[g] = sb.tile([P, PASSES2, 2, P, PACK], BF16, name="w2_bf", tag="stage%d" % (g % 2), align_bytes=64)
             src = w2_raw[b][:, :, c * 512 : (c + 1) * 512].rearrange("p j (m t) -> p m j t", t=PACK)
             nc.scalar.copy(w2_bf[g][:, b].rearrange("p u m j -> p m j u"), src[:, :, :, 2 * tp : 2 * tp + 2])
 
@@ -207,7 +217,12 @@ def tile_list_beetle_trap_pairs_kernel(
             scale_edge(s)
             if s + 2 < SLICES:
                 features(s + 2)
-            pick_interior(s)
+            if s + 1 < SLICES:
+                pick_interior(s, 0, 1)
+            else:
+                pick_interior(s, 0, 2)
+                weave_x(1, nc.scalar.copy, 0, 2)
+                pick_interior(s, 1, 2)
             if s == 2:
                 round_w2(0, 0)
             if s == 4:
@@ -225,7 +240,7 @@ def tile_list_beetle_trap_pairs_kernel(
         def stage2_pass(s, b):
             g, u = divmod(s, 2)
             if b == 0:
-                acc2[s] = bank(s, "acc2")
+                acc2[s] = bank((halves * RING + s) % 8, "acc2")
             cols = slice((2 * b + u) * P, (2 * b + u + 1) * P)
             nc.tensor.matmul_mx(
                 out=acc2[s][:],
@@ -248,24 +263,22 @@ def tile_list_beetle_trap_pairs_kernel(
         cand3, cand4 = {}, {}
 
         def pick_candidates(s):
-            g, u = divmod(s, 2)
-            if u == 0:
-                cand3[g] = sb.tile([P, 2, KEPT], F32, name="cand3", bufs=2)
-                cand4[g] = sb.tile([P, 2, KEPT], F32, name="cand4", bufs=2)
-            nc.vector.tensor_copy(cand3[g][:, u, :], y[s][:].indirect(pos3_t[:]))
-            nc.vector.tensor_copy(cand4[g][:, u, :], y[s][:].indirect(pos4_t[:]))
+            cand3[s] = sb.tile([P, KEPT], F32, name="cand3", bufs=2)
+            cand4[s] = sb.tile([P, KEPT], F32, name="cand4", bufs=2)
+            nc.vector.tensor_copy(cand3[s][:], y[s][:].indirect(pos3_t[:]))
+            nc.vector.tensor_copy(cand4[s][:], y[s][:].indirect(pos4_t[:]))
 
-        out_rows = out.rearrange("(c p t) j -> c p t j", p=P, t=PACK)
+        out_rows = out.rearrange("(c p t) j -> c t p j", p=P, t=PACK)
 
-        def lesser(g):
-            c, tp = divmod(g, 2)
-            res = sb.tile([P, 2, KEPT], F32, name="res", bufs=2)
-            nc.vector.tensor_tensor(res[:], cand3[g][:], cand4[g][:], ALU.min)
-            nc.sync.dma_start(out_rows[c][:, 2 * tp : 2 * tp + 2, :], res[:])
+        def lesser(s):
+            c, t = divmod(s, PACK)
+            res = sb.tile([P, KEPT], F32, name="res", bufs=4)
+            nc.vector.tensor_tensor(res[:], cand3[s][:], cand4[s][:], ALU.min)
+            nc.sync.dma_start(out_rows[c][t], res[:])
 
         stage2_pass(0, 0)
         stage2_pass(1, 0)
-        weave_x(1, nc.vector.tensor_copy, 0, 1)
+        weave_x(1, nc.vector.tensor_copy, 1, 2)
         round_w2(1, 1)
         quantise_x(1)
         quantise_w2(1)
@@ -283,9 +296,9 @@ def tile_list_beetle_trap_pairs_kernel(
                 round_w2(g + 2, u)
             if s + 1 < SLICES:
                 add_skip(s + 1)
-            if u == 0 and g > 0:
-                lesser(g - 1)
+            if s > 0:
+                lesser(s - 1)
             pick_candidates(s)
             if u == 1 and g + 2 < groups:
                 quantise_w2(g + 2)
-        lesser(groups - 1)
+        lesser(SLICES - 1)

from contextlib import ExitStack

import concourse.mybir as mybir

K, T, S, H, PAIRS, KEPT = 1536, 4096, 1024, 1024, 512, 256
FLOPS = 2 * K * H * S + 2 * H * H * PAIRS

F32 = mybir.dt.float32
BF16 = mybir.dt.bfloat16
I32 = mybir.dt.int32
U32 = mybir.dt.uint32
U16 = mybir.dt.uint16
U8 = mybir.dt.uint8
FP8X4 = mybir.dt.float8_e4m3fn_x4
FP4X4 = mybir.dt.float4_e2m1fn_x4
ALU = mybir.AluOpType
ACT = mybir.ActivationFunctionType

P = 128
PACK = 4
BANK = 512
PASSES1 = K // (P * PACK)
PASSES2 = H // (P * PACK)
SLICES = H // P
QUADS = 4
AHEAD = 3
RING = 3


def tile_list_beetle_trap_pairs_kernel(
    tc, tab_words, tab_scales, offs, pos1, pos2, pos3, pos4, w1_words, w1_scales, gain, w2, gr, out
):
    nc = tc.nc
    with ExitStack() as ctx:
        lists = ctx.enter_context(tc.tile_pool(name="lists", bufs=1))
        sb = ctx.enter_context(tc.tile_pool(name="sb", bufs=1))
        psum = ctx.enter_context(tc.psum_pool(name="psum", bufs=1))

        def load_list(src, name):
            t = lists.tile(list(src.shape), U16, name=name)
            nc.sync.dma_start(t[:], src)
            return t

        def bank(index, name):
            return psum.tile([P, BANK], F32, name=name, tag="bank%d" % index)

        tab_sc_win = sb.tile([P, T], U8, name="tab_sc_win", tag="picked0", align_bytes=64)
        w1_sc_raw = sb.tile([P, H], U8, name="w1_sc_raw", align_bytes=64)
        first_row = 48
        end_row = first_row + 16 * PASSES1
        for raw in (tab_sc_win, w1_sc_raw):
            nc.vector.memset(raw[:first_row, :].bitcast(I32), 0)
            nc.vector.memset(raw[end_row:, :].bitcast(I32), 0)
        planes = sb.tile([P, PASSES1, S + H], U8, name="planes", align_bytes=64)
        nc.vector.memset(planes[:].rearrange("p a n -> p (a n)").bitcast(I32), 0)

        packed_rows = slice(first_row, end_row)
        offs_t = load_list(offs, "offs_t")
        nc.scalar.dma_start(tab_sc_win[packed_rows, :].bitcast(I32), tab_scales.rearrange("a q n -> q a n").bitcast(I32))
        w1_raw = sb.tile([P, PASSES1, 2 * H], U8, name="w1_raw", align_bytes=64)
        nc.sync.dma_start(w1_raw[:].bitcast(I32), w1_words.rearrange("a p n -> p a n").bitcast(I32))
        nc.sync.dma_start(w1_sc_raw[packed_rows, :].bitcast(I32), w1_scales.rearrange("a q n -> q a n").bitcast(I32))
        windows = []

        def load_window(a):
            win = sb.tile([P, T], I32, name="win%d" % a, tag="big%d" % a, align_bytes=64)
            nc.sync.dma_start(win[:], tab_words[a].rearrange("p t i -> p (t i)").bitcast(I32))
            windows.append(win)

        pos1_t = load_list(pos1, "pos1_t")
        pos2_t = load_list(pos2, "pos2_t")
        pos3_t = load_list(pos3, "pos3_t")
        load_window(0)
        pos4_t = load_list(pos4, "pos4_t")
        load_window(1)
        gain_t = sb.tile([P, PASSES2, PACK], F32, name="gain_t")
        nc.gpsimd.dma_start(gain_t[:], gain.rearrange("(b p t) -> p b t", p=P, t=PACK))
        gr_t = sb.tile([P, PASSES2, PACK], F32, name="gr_t")
        nc.gpsimd.dma_start(gr_t[:], gr.rearrange("(b p t) -> p b t", p=P, t=PACK))

        v_sc_picked = sb.tile([P, S], U8, name="v_sc_picked", tag="big2", align_bytes=64)
        nc.vector.tensor_copy(v_sc_picked[:], tab_sc_win[:].indirect(offs_t[:]))
        packed = sb.tile([P, S + H], U8, name="packed", align_bytes=64)
        nc.vector.tensor_copy(
            packed[:, S:].rearrange("p (b t q) -> p b t q", b=PASSES2, t=PACK),
            w1_sc_raw[:].rearrange("p (b q t) -> p b t q", b=PASSES2, t=PACK),
        )
        nc.vector.tensor_copy(packed[:, :S].bitcast(I32), v_sc_picked[:].bitcast(I32))
        rows = 4 * PASSES1
        for q in range(QUADS):
            (nc.scalar if q % 2 == 0 else nc.sync).dma_start(
                planes[32 * q : 32 * q + 4, :, :].bitcast(I32),
                packed[first_row + rows * q : first_row + rows * (q + 1), :].bitcast(I32),
            )
        load_window(PASSES1 - 1)

        w1_codes = sb.tile([P, PASSES1, 2 * H], U8, name="w1_codes", align_bytes=64)
        for a in range(PASSES1):
            nc.vector.tensor_copy(
                w1_codes[:, a, :].bitcast(U16).rearrange("p (b t q) -> p b t q", b=PASSES2, t=PACK),
                w1_raw[:, a, :].bitcast(U16).rearrange("p (b q t) -> p b t q", b=PASSES2, t=PACK),
            )

        gain_sq = sb.tile([P, SLICES], F32, name="gain_sq")
        skip_k = sb.tile([P, SLICES], F32, name="skip_k")
        flat_gain = gain_t[:].rearrange("p b t -> p (b t)")
        nc.gpsimd.tensor_tensor(gain_sq[:], flat_gain, flat_gain, ALU.mult)
        nc.gpsimd.tensor_tensor(skip_k[:], flat_gain, gr_t[:].rearrange("p b t -> p (b t)"), ALU.mult)

        halves = S // BANK
        cols16 = BANK // 16
        v_words = [sb.tile([P, S], U32, name="v_words%d" % a, tag="picked%d" % a, align_bytes=64) for a in range(PASSES1)]
        acc1 = {}

        def stage1_pass(s, h, a):
            if a == 0:
                acc1[s, h] = bank(halves * (s % RING) + h, "acc1")
            cols = slice(h * BANK, (h + 1) * BANK)
            nc.tensor.matmul_mx(
                out=acc1[s, h][:],
                lhsT=w1_codes[:, a, 2 * P * s : 2 * P * (s + 1)].bitcast(FP4X4),
                lhsT_scale=planes[:, a, S + P * s : S + P * (s + 1)],
                rhs=v_words[a][:, cols].bitcast(FP8X4),
                rhs_scale=planes[:, a, cols],
                start=(a == 0),
                stop=(a == PASSES1 - 1),
            )

        last = PASSES1 - 1
        for a in range(last):
            nc.vector.tensor_copy(v_words[a][:], windows[a][:].bitcast(U32).indirect(offs_t[:]))
            for s in range(AHEAD):
                for h in range(halves):
                    stage1_pass(s, h, a)
        for h in range(halves):
            nc.vector.tensor_copy(
                v_words[last][:, h * BANK : (h + 1) * BANK],
                windows[last][:].bitcast(U32).indirect(offs_t[:, h * cols16 : (h + 1) * cols16]),
            )

        w2_raw = []
        for b in range(PASSES2):
            raw = sb.tile([P, PACK, H], F32, name="w2_raw%d" % b, tag="big%d" % (b + 1), align_bytes=64)
            nc.sync.dma_start(raw[:], w2[b * 512 : (b + 1) * 512, :].rearrange("(p j) n -> p j n", j=PACK))
            w2_raw.append(raw)

        tanh1, edge, edge_g2 = {}, {}, {}
        x_f32 = [sb.tile([P, PACK, PAIRS], F32, name="x_f32_%d" % b) for b in range(PASSES2)]
        x_bf = [sb.tile([P, PAIRS, PACK], BF16, name="x_bf%d" % b, align_bytes=64) for b in range(PASSES2)]
        x_codes = [sb.tile([P, PAIRS], U32, name="x_codes%d" % b, align_bytes=64) for b in range(PASSES2)]
        x_sc = [sb.tile([P, PAIRS], U8, name="x_sc%d" % b, align_bytes=64) for b in range(PASSES2)]

        def features(s):
            for h in range(halves):
                for a in range(last if s < AHEAD else 0, PASSES1):
                    stage1_pass(s, h, a)
            if s < 2:
                tanh1[s] = sb.tile([P, S], F32, name="tanh1", tag="stage%d" % s, align_bytes=64)
            else:
                tanh1[s] = sb.tile([P, S], F32, name="tanh1", bufs=3)
            for h in range(halves):
                nc.scalar.activation(tanh1[s][:, h * BANK : (h + 1) * BANK], acc1[s, h][:], ACT.Tanh)

        def pick_edge(s):
            edge[s] = sb.tile([P, PAIRS], F32, name="edge%d" % s)
            nc.vector.tensor_copy(edge[s][:], tanh1[s][:].indirect(pos1_t[:]))

        def scale_edge(s):
            edge_g2[s] = sb.tile([P, PAIRS], F32, name="edge_g2", bufs=3)
            nc.scalar.activation(edge_g2[s][:], edge[s][:], ACT.Copy, scale=gain_sq[:, s : s + 1])

        def pick_interior(s, part, parts):
            b, t = divmod(s, PACK)
            w = PAIRS // parts
            cols = slice(part * w, (part + 1) * w)
            entries = pos2_t[:, part * w // 16 : (part + 1) * w // 16]
            nc.vector.tensor_tensor(x_f32[b][:, t, cols], tanh1[s][:].indirect(entries), edge_g2[s][:, cols], ALU.mult)

        def weave_x(b, engine_copy, part, parts):
            w = PAIRS // parts
            cols = slice(part * w, (part + 1) * w)
            engine_copy(
                x_bf[b][:, cols, :].rearrange("p (c i) t -> p c t i", i=4),
                x_f32[b][:, :, cols].rearrange("p t (c i) -> p c t i", i=4),
            )

        def quantise_x(b):
            nc.vector.quantize_mx(
                out=x_codes[b][:].bitcast(FP8X4), scales=x_sc[b][:], in_=x_bf[b][:].rearrange("p m t -> p (m t)")
            )

        groups = SLICES // 2
        w2_bf, w2_codes, w2_sc = {}, {}, {}

        def round_w2(g, b):
            c, tp = divmod(g, 2)
            if b == 0:
                w2_bf[g] = sb.tile([P, PASSES2, 2, P, PACK], BF16, name="w2_bf", tag="stage%d" % (g % 2), align_bytes=64)
            src = w2_raw[b][:, :, c * 512 : (c + 1) * 512].rearrange("p j (m t) -> p m j t", t=PACK)
            nc.scalar.copy(w2_bf[g][:, b].rearrange("p u m j -> p m j u"), src[:, :, :, 2 * tp : 2 * tp + 2])

        def quantise_w2(g):
            w2_codes[g] = sb.tile([P, PASSES2 * 2 * P], U32, name="w2_codes%d" % g, align_bytes=64)
            w2_sc[g] = sb.tile([P, PASSES2 * 2 * P], U8, name="w2_sc%d" % g, align_bytes=64)
            nc.vector.quantize_mx(
                out=w2_codes[g][:].bitcast(FP8X4),
                scales=w2_sc[g][:],
                in_=w2_bf[g][:].rearrange("p b u m j -> p (b u m j)"),
            )

        features(0)
        features(1)
        pick_edge(0)
        for s in range(SLICES):
            if s + 1 < SLICES:
                pick_edge(s + 1)
            scale_edge(s)
            if s + 2 < SLICES:
                features(s + 2)
            if s + 1 < SLICES:
                pick_interior(s, 0, 1)
            else:
                pick_interior(s, 0, 2)
                weave_x(1, nc.scalar.copy, 0, 2)
                pick_interior(s, 1, 2)
            if s == 2:
                round_w2(0, 0)
            if s == 4:
                weave_x(0, nc.scalar.copy, 0, 2)
            if s == 5:
                weave_x(0, nc.scalar.copy, 1, 2)
                round_w2(0, 1)
            if s == 6:
                quantise_x(0)
                quantise_w2(0)
                round_w2(1, 0)

        acc2, pair, y = {}, {}, {}

        def stage2_pass(s, b):
            g, u = divmod(s, 2)
            if b == 0:
                acc2[s] = bank((halves * RING + s) % 8, "acc2")
            cols = slice((2 * b + u) * P, (2 * b + u + 1) * P)
            nc.tensor.matmul_mx(
                out=acc2[s][:],
                lhsT=w2_codes[g][:, cols].bitcast(FP8X4),
                lhsT_scale=w2_sc[g][:, cols],
                rhs=x_codes[b][:].bitcast(FP8X4),
                rhs_scale=x_sc[b][:],
                start=(b == 0),
                stop=(b == PASSES2 - 1),
            )

        def pair_features(s):
            pair[s] = sb.tile([P, PAIRS], F32, name="pair", bufs=3)
            nc.scalar.activation(pair[s][:], acc2[s][:], ACT.Tanh)

        def add_skip(s):
            y[s] = sb.tile([P, PAIRS], F32, name="y", bufs=3)
            nc.vector.scalar_tensor_tensor(y[s][:], edge[s][:], skip_k[:, s : s + 1], pair[s][:], ALU.mult, ALU.add)

        cand3, cand4 = {}, {}

        def pick_candidates(s):
            cand3[s] = sb.tile([P, KEPT], F32, name="cand3", bufs=2)
            cand4[s] = sb.tile([P, KEPT], F32, name="cand4", bufs=2)
            nc.vector.tensor_copy(cand3[s][:], y[s][:].indirect(pos3_t[:]))
            nc.vector.tensor_copy(cand4[s][:], y[s][:].indirect(pos4_t[:]))

        out_rows = out.rearrange("(c p t) j -> c t p j", p=P, t=PACK)

        def lesser(s):
            c, t = divmod(s, PACK)
            res = sb.tile([P, KEPT], F32, name="res", bufs=4)
            nc.vector.tensor_tensor(res[:], cand3[s][:], cand4[s][:], ALU.min)
            nc.sync.dma_start(out_rows[c][t], res[:])

        stage2_pass(0, 0)
        stage2_pass(1, 0)
        weave_x(1, nc.vector.tensor_copy, 1, 2)
        round_w2(1, 1)
        quantise_x(1)
        quantise_w2(1)
        for s in range(2):
            stage2_pass(s, 1)
            pair_features(s)
        add_skip(0)
        for s in range(SLICES):
            g, u = divmod(s, 2)
            if s + 2 < SLICES:
                stage2_pass(s + 2, 0)
                stage2_pass(s + 2, 1)
                pair_features(s + 2)
            if g + 2 < groups:
                round_w2(g + 2, u)
            if s + 1 < SLICES:
                add_skip(s + 1)
            if s > 0:
                lesser(s - 1)
            pick_candidates(s)
            if u == 1 and g + 2 < groups:
                quantise_w2(g + 2)
        lesser(SLICES - 1)
